import numpy as np
import ml_dtypes


def mxq(x, axis, fmt="e4m3"):
    dtype, down = {"e4m3": (ml_dtypes.float8_e4m3fn, 7), "e5m2": (ml_dtypes.float8_e5m2, 14)}[fmt]
    v = np.moveaxis(np.asarray(x, np.float32).astype(ml_dtypes.bfloat16).astype(np.float64), axis, -1)
    blocks = v.reshape(v.shape[:-1] + (-1, 32))
    amax = np.abs(blocks).max(-1, keepdims=True)
    byte = np.maximum(np.where(amax > 0, np.frexp(amax)[1] - 1 + 127, 0) - down, 1)
    scale = np.exp2(byte - 127.0)
    codes = (blocks / scale).astype(np.float32).astype(dtype).astype(np.float64)
    return np.moveaxis((codes * scale).reshape(v.shape), -1, axis)


WIDE = False


def mx_kscale(k):
    if not WIDE:
        return np.ones(k)
    levels = np.array([10, -10, 5, -5, 0])
    if k % 512:
        return np.exp2(np.random.permutation(np.resize(levels, k // 32))).repeat(32)
    a = np.empty((k // 512, 16))
    for p in range(k // 512):
        a[p, :8] = np.random.permutation(np.resize(levels, 8))
        for g in range(8):
            far = levels[np.abs(levels - a[p, g]) >= 10]
            a[p, g + 8] = far[np.random.randint(len(far))]
    return np.exp2(a.ravel()).repeat(32)


def f64(x):
    return np.asarray(x).astype(np.float64)


def striped(idx):
    return np.tile(idx.reshape(-1, 16).T, (8, 1)).astype(np.uint16)


def unstriped(offs):
    return offs[:16].T.reshape(-1).astype(np.int64)


E2M1 = np.array([0.0, 0.5, 1.0, 1.5, 2.0, 3.0, 4.0, 6.0, -0.0, -0.5, -1.0, -1.5, -2.0, -3.0, -4.0, -6.0])


def pack_weight(w, fmt):
    k, n = w.shape
    w = f64(np.asarray(w, np.float32).astype(ml_dtypes.bfloat16)).reshape(k // 32, 32, n)
    amax = np.abs(w).max(1)
    if fmt == "e4m3":
        byte = np.frexp(amax)[1] - 1 + 127 - 7
    else:
        mant, ex = np.frexp(amax / 6.0)
        byte = np.where(mant > 0.5, ex, ex - 1) + 127
    byte = np.clip(np.where(amax > 0, byte, 1), 1, 254)
    scaled = (w * np.exp2(127.0 - byte)[:, None, :]).reshape(k, n).astype(np.float32)
    by_word = np.ascontiguousarray(scaled.reshape(k // 512, 128, 4, n).transpose(0, 1, 3, 2))
    if fmt == "e4m3":
        words = by_word.astype(ml_dtypes.float8_e4m3fn).view(np.uint8)
    else:
        c = by_word.astype(ml_dtypes.float4_e2m1fn).view(np.uint8) & 0xF
        words = (c[..., 0::2] | (c[..., 1::2] << 4)).reshape(k // 512, 128, 2 * n)
    return np.ascontiguousarray(words), np.ascontiguousarray(byte.astype(np.uint8).reshape(k // 512, 16, n))


def unpack_weight(words, scales, fmt):
    g, _, n = scales.shape
    words = np.ascontiguousarray(words).reshape(g, 128, n, -1)
    if fmt == "e4m3":
        vals = words.view(ml_dtypes.float8_e4m3fn).astype(np.float64)
    else:
        nib = np.empty((g, 128, n, 4), np.uint8)
        nib[..., 0::2] = words & 0xF
        nib[..., 1::2] = words >> 4
        vals = E2M1[nib]
    vals = vals * np.repeat(np.exp2(scales.astype(np.float64) - 127.0), 8, axis=1)[..., None]
    return vals.transpose(0, 1, 3, 2).reshape(g * 512, n)


def gelu(v):
    return 0.5 * v * (1.0 + np.tanh(np.sqrt(2.0 / np.pi) * (v + 0.044715 * v**3)))


K, H, N, T, S, T2 = 1024, 512, 256, 2048, 1024, 2048

def setup_inputs():
    n = np.random.standard_normal
    s = mx_kscale(K)[:, None]
    u = mx_kscale(H)[:, None]
    tab_words, tab_scales = pack_weight(n((K, T)) * s, "e4m3")
    tab2_words, tab2_scales = pack_weight(n((K, T)) * s, "e4m3")
    w1_words, w1_scales = pack_weight(n((K, H)) / np.sqrt(K) / s, "e2m1")
    w3_words, w3_scales = pack_weight(n((K, H)) / np.sqrt(K) / s * u.T, "e4m3")
    perm = np.random.permutation(T2)
    return {
        "tab_words": tab_words, "tab_scales": tab_scales,
        "tab2_words": tab2_words, "tab2_scales": tab2_scales,
        "w1_words": w1_words, "w1_scales": w1_scales,
        "w2": (n((K, H)) / np.sqrt(K) / s).astype(np.float32),
        "w3_words": w3_words, "w3_scales": w3_scales,
        "w4": (n((H, N)) / np.sqrt(H) / u).astype(np.float32),
        "gain": (0.6 * np.exp(0.3 * n(H)) * u[:, 0]).astype(np.float32),
        "mean": (0.5 * n(H) * u[:, 0]).astype(np.float32),
        "wg1": np.exp(0.3 * n((128, S))).astype(np.float32),
        "wg2": np.exp(0.3 * n((128, S))).astype(np.float32),
        "offs": striped(np.random.permutation(T)[:S]),
        "offs2": striped(np.random.permutation(T)[:S]),
        "offs3": striped(perm[:S]), "offs4": striped(perm[S:]),
    }

def reference(tab_words, tab_scales, tab2_words, tab2_scales, w1_words, w1_scales, w2, w3_words, w3_scales, w4, gain, mean, wg1, wg2, offs, offs2, offs3, offs4):
    v = unpack_weight(tab_words, tab_scales, "e4m3")[:, unstriped(offs)]
    v2 = unpack_weight(tab2_words, tab2_scales, "e4m3")[:, unstriped(offs2)]
    a = unpack_weight(w1_words, w1_scales, "e2m1").T @ v
    h1 = f64(gain)[:, None] * (a * np.abs(a))
    b = mxq(f64(w2), 0, "e4m3").T @ v2
    d = unpack_weight(w3_words, w3_scales, "e4m3").T @ v2
    h2 = np.tanh(b) * d
    page = np.zeros((H, T2))
    page[:, unstriped(offs3)] = np.tile(f64(wg1), (H // 128, 1)) * h1
    page[:, unstriped(offs4)] = np.tile(f64(wg2), (H // 128, 1)) * h2
    z = page - f64(mean)[:, None]
    return mxq(f64(w4), 0, "e4m3").T @ mxq(z, 0, "e4m3")

@@ -1,0 +1,251 @@
+from contextlib import ExitStack
+
+import concourse.mybir as mybir
+
+K, H, N, T, S, T2 = 1024, 512, 256, 2048, 1024, 2048
+FLOPS = 2 * (3 * K * H * S + H * N * T2)
+
+F32 = mybir.dt.float32
+BF16 = mybir.dt.bfloat16
+I32 = mybir.dt.int32
+U32 = mybir.dt.uint32
+U16 = mybir.dt.uint16
+U8 = mybir.dt.uint8
+FP8X4 = mybir.dt.float8_e4m3fn_x4
+FP4X4 = mybir.dt.float4_e2m1fn_x4
+ACT = mybir.ActivationFunctionType
+ALU = mybir.AluOpType
+
+P = 128
+PACK = 4
+PASSES = K // (P * PACK)
+BANK = 512
+QUADS = 4
+
+
+def tile_list_subgrid_closure_weave_kernel(
+    tc, tab_words, tab_scales, tab2_words, tab2_scales, w1_words, w1_scales, w2, w3_words, w3_scales,
+    w4, gain, mean, wg1, wg2, offs, offs2, offs3, offs4, out,
+):
+    nc = tc.nc
+    with ExitStack() as ctx:
+        held = ctx.enter_context(tc.tile_pool(name="held", bufs=1))
+        ring = ctx.enter_context(tc.tile_pool(name="ring", bufs=4))
+        psum = ctx.enter_context(tc.psum_pool(name="psum", bufs=2))
+
+        def tile(shape, dtype, name):
+            return held.tile(shape, dtype, name=name, align_bytes=64)
+
+        def load_list(src, name):
+            dst = held.tile([P, S // 16], U16, name=name)
+            nc.sync.dma_start(dst[:], src)
+            return dst
+
+        def zeroed(shape, name, engine):
+            dst = tile(shape, U8, name)
+            engine.memset(dst[:].bitcast(I32), 0)
+            return dst
+
+        def load_words(src, a, name, queue):
+            dst = ring.tile([P, T], I32, name=name, tag="wide", align_bytes=64)
+            queue.dma_start(dst[:], src[a].rearrange("p n i -> p (n i)").bitcast(I32))
+            return dst
+
+        def load_packed_scales(dst, src, queue):
+            for q in range(QUADS):
+                queue.dma_start(dst[32 * q : 32 * q + 4 * PASSES, :].bitcast(I32), src[:, 4 * q : 4 * q + 4, :].bitcast(I32))
+
+        def gather(window, lst, dtype, name):
+            dst = tile([P, S], dtype, name)
+            nc.vector.tensor_copy(dst[:], window.indirect(lst[:]))
+            return dst
+
+        def load_weave(src, t, name, queue):
+            dst = tile([P, S], F32, name)
+            rows = src.rearrange("(q t) j -> t q j", t=PACK)[t]
+            queue.dma_start(dst[:], rows.unsqueeze(0).to_broadcast([QUADS, 32, S]))
+            return dst
+
+        tab_s = zeroed([P, T], "tab_s", nc.vector)
+        load_packed_scales(tab_s, tab_scales, nc.scalar)
+        w1_s_raw = zeroed([P, PASSES * H], "w1_s_raw", nc.vector)
+        tab2_s = zeroed([P, T], "tab2_s", nc.vector)
+        w3_s_raw = zeroed([P, H], "w3_s_raw", nc.vector)
+        v_s_hi = zeroed([P, S], "v_s_hi", nc.vector)
+
+        idx = load_list(offs, "idx")
+        tab_w = [load_words(tab_words, 0, "tab_w0", nc.sync)]
+        w1_raw = tile([P, PASSES, 2 * H], U8, "w1_raw")
+        nc.sync.dma_start(w1_raw[:].bitcast(I32), w1_words.rearrange("a p c -> p a c").bitcast(I32))
+        tab_w.append(load_words(tab_words, 1, "tab_w1", nc.sync))
+        for q in range(QUADS):
+            nc.sync.dma_start(
+                w1_s_raw[32 * q : 32 * q + 4, :].rearrange("r (a c) -> r a c", a=PASSES).bitcast(I32),
+                w1_scales[:, 4 * q : 4 * q + 4, :].rearrange("a r c -> r a c").bitcast(I32),
+            )
+        gain_c = tile([P, PACK], F32, "gain_c")
+        nc.sync.dma_start(gain_c[:], gain.rearrange("(p t) -> p t", t=PACK))
+        weave1 = [load_weave(wg1, 0, "weave1_0", nc.sync)]
+        idx2 = load_list(offs2, "idx2")
+        tab2_w = [load_words(tab2_words, a, "tab2_w%d" % a, nc.sync) for a in range(PASSES)]
+        load_packed_scales(tab2_s, tab2_scales, nc.sync)
+        idx3 = load_list(offs3, "idx3")
+        weave1.append(load_weave(wg1, 1, "weave1_1", nc.sync))
+        w2_raw = []
+        for a in range(PASSES):
+            w2_raw.append(tile([P, PACK, H], F32, "w2_raw%d" % a))
+            nc.sync.dma_start(w2_raw[a][:], w2[512 * a : 512 * (a + 1), :].rearrange("(p j) c -> p j c", j=PACK))
+        weave1.extend(load_weave(wg1, t, "weave1_%d" % t, nc.sync) for t in range(2, PACK))
+        w3_raw = tile([P, PASSES, H], I32, "w3_raw")
+        nc.sync.dma_start(w3_raw[:], w3_words.rearrange("a p c i -> p a (c i)").bitcast(I32))
+        load_packed_scales(w3_s_raw, w3_scales, nc.sync)
+        idx4 = load_list(offs4, "idx4")
+        weave2 = [load_weave(wg2, t, "weave2_%d" % t, nc.sync) for t in range(PACK)]
+        mean_c = tile([P, PACK], F32, "mean_c")
+        nc.sync.dma_start(mean_c[:], mean.rearrange("(p t) -> p t", t=PACK))
+        w4_raw = tile([P, PACK, N], F32, "w4_raw")
+        nc.sync.dma_start(w4_raw[:], w4.rearrange("(p j) n -> p j n", j=PACK))
+
+        v_s = gather(tab_s[:], idx, U8, "v_s")
+        nc.scalar.dma_start(v_s_hi[0 : P - 4, :].bitcast(I32), v_s[4:P, :].bitcast(I32))
+        v_w = [gather(tab_w[0][:].bitcast(U32), idx, U32, "v_w0")]
+        w1_w = tile([P, PASSES, 2 * H], U8, "w1_w")
+        nc.vector.tensor_copy(
+            w1_w[:].bitcast(U16).rearrange("p a (t m) -> p a t m", t=PACK),
+            w1_raw[:].bitcast(U16).rearrange("p a (m t) -> p a t m", t=PACK),
+        )
+        w1_s = tile([P, PASSES, H], U8, "w1_s")
+        nc.vector.tensor_copy(
+            w1_s[:].rearrange("p a (t m) -> p a t m", t=PACK),
+            w1_s_raw[:].rearrange("p (a m t) -> p a t m", a=PASSES, t=PACK),
+        )
+        v_w.append(gather(tab_w[1][:].bitcast(U32), idx, U32, "v_w1"))
+        v2_s = gather(tab2_s[:], idx2, U8, "v2_s")
+        v2_w = [gather(tab2_w[a][:].bitcast(U32), idx2, U32, "v2_w%d" % a) for a in range(PASSES)]
+        w3_w = tile([P, PASSES, H], I32, "w3_w")
+        nc.vector.tensor_copy(
+            w3_w[:].rearrange("p a (t c i) -> p a c t i", t=PACK, i=4),
+            w3_raw[:].rearrange("p a (c i t) -> p a c t i", t=PACK, i=4),
+        )
+        w3_s = tile([P, H], U8, "w3_s")
+        nc.vector.tensor_copy(
+            w3_s[:].rearrange("p (t m) -> p t m", t=PACK),
+            w3_s_raw[:].rearrange("p (m t) -> p t m", t=PACK),
+        )
+
+        w2_w, w2_s = [], []
+        for a in range(PASSES):
+            grouped = held.tile([P, H * PACK], BF16, name="w2_g%d" % a, tag="page%d" % (a + 1), align_bytes=64)
+            nc.scalar.copy(
+                grouped[:].rearrange("p (t m j) -> p m t j", t=PACK, j=PACK),
+                w2_raw[a][:].rearrange("p j (m t) -> p m t j", t=PACK),
+            )
+            w2_w.append(tile([P, H], U32, "w2_w%d" % a))
+            w2_s.append(tile([P, H], U8, "w2_s%d" % a))
+            nc.vector.quantize_mx(out=w2_w[a][:].bitcast(FP8X4), scales=w2_s[a][:], in_=grouped[:])
+
+        pages = [tile([P, T2], F32, "page%d" % t) for t in range(PACK)]
+        neg_mean = tile([P, PACK], F32, "neg_mean")
+        nc.scalar.activation(neg_mean[:], mean_c[:], ACT.Copy, scale=-1.0)
+
+        def product(tag, cols, lhs_codes, lhs_scales, rhs_codes, rhs_scales):
+            acc = psum.tile([P, BANK], F32, name=tag)
+            for a in range(PASSES):
+                nc.tensor.matmul_mx(
+                    out=acc[:], lhsT=lhs_codes[a], lhsT_scale=lhs_scales[a],
+                    rhs=rhs_codes[a][:, cols].bitcast(FP8X4), rhs_scale=rhs_scales[a][:, cols],
+                    start=(a == 0), stop=(a == PASSES - 1),
+                )
+            return acc
+
+        def stream1(t):
+            ch = slice(P * t, P * (t + 1))
+            codes = [w1_w[:, a, 2 * P * t : 2 * P * (t + 1)].bitcast(FP4X4) for a in range(PASSES)]
+            scales = [w1_s[:, a, ch] for a in range(PASSES)]
+
+            for j0 in range(0, S, BANK):
+                cols = slice(j0, j0 + BANK)
+                acc = product("acc_a", cols, codes, scales, v_w, [v_s[:], v_s_hi[:]])
+                mag = ring.tile([P, BANK], F32, name="u")
+                nc.scalar.activation(mag[:], acc[:], ACT.Abs)
+                lin = ring.tile([P, BANK], F32, name="v")
+                nc.scalar.activation(lin[:], acc[:], ACT.Copy, scale=gain_c[:, t : t + 1])
+                nc.gpsimd.tensor_tensor(weave1[t][:, cols], weave1[t][:, cols], mag[:], ALU.mult)
+                nc.gpsimd.tensor_tensor(weave1[t][:, cols], weave1[t][:, cols], lin[:], ALU.mult)
+            nc.vector.tensor_copy(pages[t][:].indirect(idx3[:]), weave1[t][:])
+
+        def stream2(t):
+            ch = slice(P * t, P * (t + 1))
+            planes = [v2_s[4 * a : P, :] for a in range(PASSES)]
+            parts = ring.tile([P, 2, S], F32, name="parts", tag="wide", align_bytes=64)
+
+            for j0 in range(0, S, BANK):
+                cols = slice(j0, j0 + BANK)
+                acc_b = product("acc_b", cols, [w2_w[a][:, ch].bitcast(FP8X4) for a in range(PASSES)],
+                                [w2_s[a][:, ch] for a in range(PASSES)], v2_w, planes)
+                acc_d = product("acc_d", cols, [w3_w[:, a, ch].bitcast(FP8X4) for a in range(PASSES)],
+                                [w3_s[4 * a : P, ch] for a in range(PASSES)], v2_w, planes)
+                nc.scalar.activation(parts[:, 0, cols], acc_b[:], ACT.Tanh)
+                nc.scalar.copy(parts[:, 1, cols], acc_d[:])
+            nc.gpsimd.tensor_tensor(weave2[t][:], weave2[t][:], parts[:, 0, :], ALU.mult)
+            nc.gpsimd.tensor_tensor(weave2[t][:], weave2[t][:], parts[:, 1, :], ALU.mult)
+            nc.vector.tensor_copy(pages[t][:].indirect(idx4[:]), weave2[t][:])
+
+        chunks = [slice(m0, m0 + BANK) for m0 in range(0, T2, BANK)]
+        z = [tile([P, BANK, PACK], BF16, "z%d" % c) for c in range(len(chunks))]
+
+        def centre_on_scalar(t, c):
+            width = 2 if t == PACK - 2 else 1
+            nc.scalar.activation(
+                z[c][:, :, t : t + width], pages[t][:, chunks[c]].unsqueeze(2).to_broadcast([P, BANK, width]),
+                ACT.Identity, bias=neg_mean[:, t : t + 1],
+            )
+
+        for t in range(PACK):
+            stream1(t)
+
+        w4_g = tile([P, N * PACK], BF16, "w4_g")
+        nc.scalar.copy(
+            w4_g[:].rearrange("p (c i j) -> p c j i", i=4, j=PACK),
+            w4_raw[:].rearrange("p j (c i) -> p c j i", i=4),
+        )
+        w4_w = tile([P, N], U32, "w4_w")
+        w4_s = tile([P, N], U8, "w4_s")
+        nc.vector.quantize_mx(out=w4_w[:].bitcast(FP8X4), scales=w4_s[:], in_=w4_g[:])
+
+        for t in range(PACK):
+            stream2(t)
+        for t in range(PACK - 1):
+            for c in range(len(chunks)):
+                centre_on_scalar(t, c)
+
+        last = PACK - 1
+        centre_on_scalar(last, len(chunks) - 1)
+
+        def centre_last(c):
+            nc.vector.tensor_scalar(z[c][:, :, last], pages[last][:, chunks[c]], mean_c[:, last : last + 1], None, ALU.subtract)
+
+        def finish(c):
+            z_w = tile([P, BANK], U32, "z_w%d" % c)
+            z_s = tile([P, BANK], U8, "z_s%d" % c)
+            nc.vector.quantize_mx(out=z_w[:].bitcast(FP8X4), scales=z_s[:], in_=z[c][:].rearrange("p m t -> p (m t)"))
+            for n0 in range(0, N, P):
+                acc = psum.tile([P, BANK], F32, name=("acc_a" if n0 else "acc_o"))
+                nc.tensor.matmul_mx(
+                    out=acc[:], lhsT=w4_w[:, n0 : n0 + P].bitcast(FP8X4), lhsT_scale=w4_s[:, n0 : n0 + P],
+                    rhs=z_w[:].bitcast(FP8X4), rhs_scale=z_s[:], start=True, stop=True,
+                )
+                res = ring.tile([P, BANK], F32, name="res")
+                if c == len(chunks) - 1 and n0:
+                    nc.vector.tensor_copy(res[:], acc[:])
+                else:
+                    nc.scalar.copy(res[:], acc[:])
+                nc.sync.dma_start(out[n0 : n0 + P, chunks[c]], res[:])
+
+        centre_last(0)
+        centre_last(1)
+        finish(0)
+        centre_last(2)
+        finish(1)
+        finish(2)
+        finish(3)

@@ -106,9 +106,10 @@ def tile_list_subgrid_closure_weave_kernel(
         w4_raw = tile([P, PACK, N], F32, "w4_raw")
         nc.sync.dma_start(w4_raw[:], w4.rearrange("(p j) n -> p j n", j=PACK))
 
-        v_s = gather(tab_s[:], idx, U8, "v_s")
-        nc.scalar.dma_start(v_s_hi[0 : P - 4, :].bitcast(I32), v_s[4:P, :].bitcast(I32))
         v_w = [gather(tab_w[0][:].bitcast(U32), idx, U32, "v_w0")]
+        v_s = ring.tile([P, S], U8, name="v_s", tag="wide", align_bytes=64)
+        nc.vector.tensor_copy(v_s[:], tab_s[:].indirect(idx[:]))
+        nc.scalar.dma_start(v_s_hi[0 : P - 4, :].bitcast(I32), v_s[4:P, :].bitcast(I32))
         w1_w = tile([P, PASSES, 2 * H], U8, "w1_w")
         nc.vector.tensor_copy(
             w1_w[:].bitcast(U16).rearrange("p a (t m) -> p a t m", t=PACK),
@@ -122,6 +123,71 @@ def tile_list_subgrid_closure_weave_kernel(
         v_w.append(gather(tab_w[1][:].bitcast(U32), idx, U32, "v_w1"))
         v2_s = gather(tab2_s[:], idx2, U8, "v2_s")
         v2_w = [gather(tab2_w[a][:].bitcast(U32), idx2, U32, "v2_w%d" % a) for a in range(PASSES)]
+        pages = [tile([P, T2], F32, "page%d" % t) for t in range(PACK)]
+        neg_mean = tile([P, PACK], F32, "neg_mean")
+        nc.scalar.activation(neg_mean[:], mean_c[:], ACT.Copy, scale=-1.0)
+
+        def product(tag, bufs, cols, lhs_codes, lhs_scales, rhs_codes, rhs_scales):
+            acc = psum.tile([P, BANK], F32, name=tag, bufs=bufs)
+            for a in range(PASSES):
+                nc.tensor.matmul_mx(
+                    out=acc[:], lhsT=lhs_codes[a], lhsT_scale=lhs_scales[a],
+                    rhs=rhs_codes[a][:, cols].bitcast(FP8X4), rhs_scale=rhs_scales[a][:, cols],
+                    start=(a == 0), stop=(a == PASSES - 1),
+                )
+            return acc
+
+        halves = [slice(j0, j0 + BANK) for j0 in range(0, S, BANK)]
+        planes2 = [v2_s[4 * a : P, :] for a in range(PASSES)]
+
+        def pair_tiles(name):
+            pairs = [ring.tile([P, 2, S], F32, name=name, tag="wide", align_bytes=64) for u in range(PACK // 2)]
+            return [pairs[t // 2][:, t % 2, :] for t in range(PACK)]
+
+        def signed_square(t):
+            ch = slice(P * t, P * (t + 1))
+            codes = [w1_w[:, a, 2 * P * t : 2 * P * (t + 1)].bitcast(FP4X4) for a in range(PASSES)]
+            scales = [w1_s[:, a, ch] for a in range(PASSES)]
+            h = ring.tile([P, S], F32, name="h", bufs=3)
+            for cols in halves:
+                acc = product("acc", 6, cols, codes, scales, v_w, [v_s[:], v_s_hi[:]])
+                nc.scalar.activation(mag[t][:, cols], acc[:], ACT.Abs)
+                nc.vector.scalar_tensor_tensor(h[:, cols], acc[:], gain_c[:, t : t + 1], mag[t][:, cols], ALU.mult, ALU.mult)
+            return h
+
+        def tanh_gate(t):
+            ch = slice(P * t, P * (t + 1))
+            for cols in halves:
+                acc = product("acc_b", 2, cols, [w2_w[a][:, ch].bitcast(FP8X4) for a in range(PASSES)],
+                              [w2_s[a][:, ch] for a in range(PASSES)], v2_w, planes2)
+                nc.scalar.activation(gate[t][:, cols], acc[:], ACT.Tanh)
+
+        def gated_product(t):
+            ch = slice(P * t, P * (t + 1))
+            h = ring.tile([P, S], F32, name="h", bufs=3)
+            for cols in halves:
+                acc = product("acc", 6, cols, [w3_w[:, a, ch].bitcast(FP8X4) for a in range(PASSES)],
+                              [w3_s[4 * a : P, ch] for a in range(PASSES)], v2_w, planes2)
+                nc.vector.tensor_tensor(h[:, cols], acc[:], gate[t][:, cols], ALU.mult)
+            return h
+
+        def scatter(t, lst, h, weave):
+            nc.vector.tensor_tensor(pages[t][:].indirect(lst[:]), h[:], weave[t][:], ALU.mult)
+
+        chunks = [slice(m0, m0 + BANK) for m0 in range(0, T2, BANK)]
+        z = [tile([P, BANK, PACK], BF16, "z%d" % c) for c in range(len(chunks))]
+
+        def centre_on_scalar(t, c):
+            width = 2 if t == PACK - 2 else 1
+            nc.scalar.activation(
+                z[c][:, :, t : t + width], pages[t][:, chunks[c]].unsqueeze(2).to_broadcast([P, BANK, width]),
+                ACT.Identity, bias=neg_mean[:, t : t + 1],
+            )
+
+        mag = pair_tiles("mag")
+        gate = pair_tiles("gate")
+        h1 = [signed_square(0), signed_square(1)]
+        scatter(0, idx3, h1[0], weave1)
         w3_w = tile([P, PASSES, H], I32, "w3_w")
         nc.vector.tensor_copy(
             w3_w[:].rearrange("p a (t c i) -> p a c t i", t=PACK, i=4),
@@ -135,7 +201,7 @@ def tile_list_subgrid_closure_weave_kernel(
 
         w2_w, w2_s = [], []
         for a in range(PASSES):
-            grouped = held.tile([P, H * PACK], BF16, name="w2_g%d" % a, tag="page%d" % (a + 1), align_bytes=64)
+            grouped = tile([P, H * PACK], BF16, "w2_g%d" % a)
             nc.scalar.copy(
                 grouped[:].rearrange("p (t m j) -> p m t j", t=PACK, j=PACK),
                 w2_raw[a][:].rearrange("p j (m t) -> p m t j", t=PACK),
@@ -144,66 +210,14 @@ def tile_list_subgrid_closure_weave_kernel(
             w2_s.append(tile([P, H], U8, "w2_s%d" % a))
             nc.vector.quantize_mx(out=w2_w[a][:].bitcast(FP8X4), scales=w2_s[a][:], in_=grouped[:])
 
-        pages = [tile([P, T2], F32, "page%d" % t) for t in range(PACK)]
-        neg_mean = tile([P, PACK], F32, "neg_mean")
-        nc.scalar.activation(neg_mean[:], mean_c[:], ACT.Copy, scale=-1.0)
-
-        def product(tag, cols, lhs_codes, lhs_scales, rhs_codes, rhs_scales):
-            acc = psum.tile([P, BANK], F32, name=tag)
-            for a in range(PASSES):
-                nc.tensor.matmul_mx(
-                    out=acc[:], lhsT=lhs_codes[a], lhsT_scale=lhs_scales[a],
-                    rhs=rhs_codes[a][:, cols].bitcast(FP8X4), rhs_scale=rhs_scales[a][:, cols],
-                    start=(a == 0), stop=(a == PASSES - 1),
-                )
-            return acc
-
-        def stream1(t):
-            ch = slice(P * t, P * (t + 1))
-            codes = [w1_w[:, a, 2 * P * t : 2 * P * (t + 1)].bitcast(FP4X4) for a in range(PASSES)]
-            scales = [w1_s[:, a, ch] for a in range(PASSES)]
-
-            for j0 in range(0, S, BANK):
-                cols = slice(j0, j0 + BANK)
-                acc = product("acc_a", cols, codes, scales, v_w, [v_s[:], v_s_hi[:]])
-                mag = ring.tile([P, BANK], F32, name="u")
-                nc.scalar.activation(mag[:], acc[:], ACT.Abs)
-                lin = ring.tile([P, BANK], F32, name="v")
-                nc.scalar.activation(lin[:], acc[:], ACT.Copy, scale=gain_c[:, t : t + 1])
-                nc.gpsimd.tensor_tensor(weave1[t][:, cols], weave1[t][:, cols], mag[:], ALU.mult)
-                nc.gpsimd.tensor_tensor(weave1[t][:, cols], weave1[t][:, cols], lin[:], ALU.mult)
-            nc.vector.tensor_copy(pages[t][:].indirect(idx3[:]), weave1[t][:])
-
-        def stream2(t):
-            ch = slice(P * t, P * (t + 1))
-            planes = [v2_s[4 * a : P, :] for a in range(PASSES)]
-            parts = ring.tile([P, 2, S], F32, name="parts", tag="wide", align_bytes=64)
-
-            for j0 in range(0, S, BANK):
-                cols = slice(j0, j0 + BANK)
-                acc_b = product("acc_b", cols, [w2_w[a][:, ch].bitcast(FP8X4) for a in range(PASSES)],
-                                [w2_s[a][:, ch] for a in range(PASSES)], v2_w, planes)
-                acc_d = product("acc_d", cols, [w3_w[:, a, ch].bitcast(FP8X4) for a in range(PASSES)],
-                                [w3_s[4 * a : P, ch] for a in range(PASSES)], v2_w, planes)
-                nc.scalar.activation(parts[:, 0, cols], acc_b[:], ACT.Tanh)
-                nc.scalar.copy(parts[:, 1, cols], acc_d[:])
-            nc.gpsimd.tensor_tensor(weave2[t][:], weave2[t][:], parts[:, 0, :], ALU.mult)
-            nc.gpsimd.tensor_tensor(weave2[t][:], weave2[t][:], parts[:, 1, :], ALU.mult)
-            nc.vector.tensor_copy(pages[t][:].indirect(idx4[:]), weave2[t][:])
-
-        chunks = [slice(m0, m0 + BANK) for m0 in range(0, T2, BANK)]
-        z = [tile([P, BANK, PACK], BF16, "z%d" % c) for c in range(len(chunks))]
-
-        def centre_on_scalar(t, c):
-            width = 2 if t == PACK - 2 else 1
-            nc.scalar.activation(
-                z[c][:, :, t : t + width], pages[t][:, chunks[c]].unsqueeze(2).to_broadcast([P, BANK, width]),
-                ACT.Identity, bias=neg_mean[:, t : t + 1],
-            )
-
+        h1.append(signed_square(2))
+        scatter(1, idx3, h1[1], weave1)
+        h1.append(signed_square(3))
         for t in range(PACK):
-            stream1(t)
-
+            tanh_gate(t)
+        scatter(2, idx3, h1[2], weave1)
+        h2 = [gated_product(0)]
+        scatter(3, idx3, h1[3], weave1)
         w4_g = tile([P, N * PACK], BF16, "w4_g")
         nc.scalar.copy(
             w4_g[:].rearrange("p (c i j) -> p c j i", i=4, j=PACK),
@@ -214,29 +228,35 @@ def tile_list_subgrid_closure_weave_kernel(
         nc.vector.quantize_mx(out=w4_w[:].bitcast(FP8X4), scales=w4_s[:], in_=w4_g[:])
 
         for t in range(PACK):
-            stream2(t)
+            if t + 1 < PACK:
+                h2.append(gated_product(t + 1))
+            scatter(t, idx4, h2[t], weave2)
         for t in range(PACK - 1):
             for c in range(len(chunks)):
                 centre_on_scalar(t, c)
 
         last = PACK - 1
-        centre_on_scalar(last, len(chunks) - 1)
+        centre_on_scalar(last, 2)
+        centre_on_scalar(last, 3)
 
         def centre_last(c):
             nc.vector.tensor_scalar(z[c][:, :, last], pages[last][:, chunks[c]], mean_c[:, last : last + 1], None, ALU.subtract)
 
-        def finish(c):
+        def quantise(c):
             z_w = tile([P, BANK], U32, "z_w%d" % c)
             z_s = tile([P, BANK], U8, "z_s%d" % c)
             nc.vector.quantize_mx(out=z_w[:].bitcast(FP8X4), scales=z_s[:], in_=z[c][:].rearrange("p m t -> p (m t)"))
+            return z_w, z_s
+
+        def finish(c, z_w, z_s):
             for n0 in range(0, N, P):
-                acc = psum.tile([P, BANK], F32, name=("acc_a" if n0 else "acc_o"))
+                acc = psum.tile([P, BANK], F32, name="acc", bufs=6)
                 nc.tensor.matmul_mx(
                     out=acc[:], lhsT=w4_w[:, n0 : n0 + P].bitcast(FP8X4), lhsT_scale=w4_s[:, n0 : n0 + P],
                     rhs=z_w[:].bitcast(FP8X4), rhs_scale=z_s[:], start=True, stop=True,
                 )
-                res = ring.tile([P, BANK], F32, name="res")
-                if c == len(chunks) - 1 and n0:
+                res = ring.tile([P, BANK], F32, name="res", bufs=8)
+                if c > 0 and n0:
                     nc.vector.tensor_copy(res[:], acc[:])
                 else:
                     nc.scalar.copy(res[:], acc[:])
@@ -244,8 +264,6 @@ def tile_list_subgrid_closure_weave_kernel(
 
         centre_last(0)
         centre_last(1)
-        finish(0)
-        centre_last(2)
-        finish(1)
-        finish(2)
-        finish(3)
+        quantised = [quantise(c) for c in range(len(chunks))]
+        for c, (z_w, z_s) in enumerate(quantised):
+            finish(c, z_w, z_s)

@@ -1,6 +1,7 @@
 from contextlib import ExitStack
 
 import concourse.mybir as mybir
+from concourse.masks import make_identity
 
 K, H, N, T, S, T2 = 1024, 512, 256, 2048, 1024, 2048
 FLOPS = 2 * (3 * K * H * S + H * N * T2)
@@ -30,11 +31,10 @@ def tile_list_subgrid_closure_weave_kernel(
     nc = tc.nc
     with ExitStack() as ctx:
         held = ctx.enter_context(tc.tile_pool(name="held", bufs=1))
-        ring = ctx.enter_context(tc.tile_pool(name="ring", bufs=4))
         psum = ctx.enter_context(tc.psum_pool(name="psum", bufs=2))
 
-        def tile(shape, dtype, name):
-            return held.tile(shape, dtype, name=name, align_bytes=64)
+        def tile(shape, dtype, name, tag=None):
+            return held.tile(shape, dtype, name=name, tag=tag or name, align_bytes=64)
 
         def load_list(src, name):
             dst = held.tile([P, S // 16], U16, name=name)
@@ -46,148 +46,137 @@ def tile_list_subgrid_closure_weave_kernel(
             engine.memset(dst[:].bitcast(I32), 0)
             return dst
 
-        def load_words(src, a, name, queue):
-            dst = ring.tile([P, T], I32, name=name, tag="wide", align_bytes=64)
-            queue.dma_start(dst[:], src[a].rearrange("p n i -> p (n i)").bitcast(I32))
+        def load_words(src, a, name):
+            dst = tile([P, T], I32, name)
+            nc.sync.dma_start(dst[:], src[a].rearrange("p n i -> p (n i)").bitcast(I32))
             return dst
 
         def load_packed_scales(dst, src, queue):
             for q in range(QUADS):
                 queue.dma_start(dst[32 * q : 32 * q + 4 * PASSES, :].bitcast(I32), src[:, 4 * q : 4 * q + 4, :].bitcast(I32))
 
+        def load_rows(src, width, name, tag=None):
+            dst = tile([P, PACK, width], F32, name, tag)
+            nc.sync.dma_start(dst[:], src.rearrange("(p j) c -> p j c", j=PACK))
+            return dst
+
+        def load_column(src, name):
+            dst = tile([P, PACK], F32, name)
+            nc.sync.dma_start(dst[:], src.rearrange("(p t) -> p t", t=PACK))
+            return dst
+
+        def load_weave(src, t, name, tag):
+            dst = tile([P, S], F32, name, tag)
+            rows = src.rearrange("(q t) j -> t q j", t=PACK)[t]
+            nc.sync.dma_start(dst[:], rows.unsqueeze(0).to_broadcast([QUADS, 32, S]))
+            return dst
+
         def gather(window, lst, dtype, name):
             dst = tile([P, S], dtype, name)
             nc.vector.tensor_copy(dst[:], window.indirect(lst[:]))
             return dst
 
-        def load_weave(src, t, name, queue):
-            dst = tile([P, S], F32, name)
-            rows = src.rearrange("(q t) j -> t q j", t=PACK)[t]
-            queue.dma_start(dst[:], rows.unsqueeze(0).to_broadcast([QUADS, 32, S]))
-            return dst
+        def quantise(grouped, width, name):
+            codes = tile([P, width], U32, name + "_w")
+            scales = tile([P, width], U8, name + "_s")
+            nc.vector.quantize_mx(out=codes[:].bitcast(FP8X4), scales=scales[:], in_=grouped)
+            return codes, scales
 
-        tab_s = zeroed([P, T], "tab_s", nc.vector)
-        load_packed_scales(tab_s, tab_scales, nc.scalar)
-        w1_s_raw = zeroed([P, PASSES * H], "w1_s_raw", nc.vector)
+        def product(acc, lhs_codes, lhs_scales, rhs_codes, rhs_scales):
+            for a in range(len(lhs_codes)):
+                nc.tensor.matmul_mx(
+                    out=acc[:], lhsT=lhs_codes[a], lhsT_scale=lhs_scales[a], rhs=rhs_codes[a], rhs_scale=rhs_scales[a],
+                    start=(a == 0), stop=(a == len(lhs_codes) - 1),
+                )
+
+        ident = tile([P, P], F32, "ident")
+        make_identity(nc, ident[:])
         tab2_s = zeroed([P, T], "tab2_s", nc.vector)
+        load_packed_scales(tab2_s, tab2_scales, nc.gpsimd)
+        tab_s = zeroed([P, T], "tab_s", nc.vector)
+        load_packed_scales(tab_s, tab_scales, nc.gpsimd)
         w3_s_raw = zeroed([P, H], "w3_s_raw", nc.vector)
+        w1_s = zeroed([P, PASSES * H], "w1_s", nc.vector)
         v_s_hi = zeroed([P, S], "v_s_hi", nc.vector)
 
-        idx = load_list(offs, "idx")
-        tab_w = [load_words(tab_words, 0, "tab_w0", nc.sync)]
-        w1_raw = tile([P, PASSES, 2 * H], U8, "w1_raw")
-        nc.sync.dma_start(w1_raw[:].bitcast(I32), w1_words.rearrange("a p c -> p a c").bitcast(I32))
-        tab_w.append(load_words(tab_words, 1, "tab_w1", nc.sync))
-        for q in range(QUADS):
-            nc.sync.dma_start(
-                w1_s_raw[32 * q : 32 * q + 4, :].rearrange("r (a c) -> r a c", a=PASSES).bitcast(I32),
-                w1_scales[:, 4 * q : 4 * q + 4, :].rearrange("a r c -> r a c").bitcast(I32),
-            )
-        gain_c = tile([P, PACK], F32, "gain_c")
-        nc.sync.dma_start(gain_c[:], gain.rearrange("(p t) -> p t", t=PACK))
-        weave1 = [load_weave(wg1, 0, "weave1_0", nc.sync)]
         idx2 = load_list(offs2, "idx2")
-        tab2_w = [load_words(tab2_words, a, "tab2_w%d" % a, nc.sync) for a in range(PASSES)]
-        load_packed_scales(tab2_s, tab2_scales, nc.sync)
-        idx3 = load_list(offs3, "idx3")
-        weave1.append(load_weave(wg1, 1, "weave1_1", nc.sync))
-        w2_raw = []
-        for a in range(PASSES):
-            w2_raw.append(tile([P, PACK, H], F32, "w2_raw%d" % a))
-            nc.sync.dma_start(w2_raw[a][:], w2[512 * a : 512 * (a + 1), :].rearrange("(p j) c -> p j c", j=PACK))
-        weave1.extend(load_weave(wg1, t, "weave1_%d" % t, nc.sync) for t in range(2, PACK))
+        tab2_w = [load_words(tab2_words, a, "tab2_w%d" % a) for a in range(PASSES)]
+        idx = load_list(offs, "idx")
+        w2_raw = [load_rows(w2[0:512, :], H, "w2_raw0")]
+        tab_w = [load_words(tab_words, 0, "tab_w0")]
+        w2_raw.append(load_rows(w2[512:1024, :], H, "w2_raw1"))
         w3_raw = tile([P, PASSES, H], I32, "w3_raw")
         nc.sync.dma_start(w3_raw[:], w3_words.rearrange("a p c i -> p a (c i)").bitcast(I32))
         load_packed_scales(w3_s_raw, w3_scales, nc.sync)
+        tab_w.append(load_words(tab_words, 1, "tab_w1"))
         idx4 = load_list(offs4, "idx4")
-        weave2 = [load_weave(wg2, t, "weave2_%d" % t, nc.sync) for t in range(PACK)]
-        mean_c = tile([P, PACK], F32, "mean_c")
-        nc.sync.dma_start(mean_c[:], mean.rearrange("(p t) -> p t", t=PACK))
-        w4_raw = tile([P, PACK, N], F32, "w4_raw")
-        nc.sync.dma_start(w4_raw[:], w4.rearrange("(p j) n -> p j n", j=PACK))
+        for q in range(QUADS):
+            nc.sync.dma_start(
+                w1_s[32 * q : 32 * q + 4, :].rearrange("r (a c) -> r a c", a=PASSES).bitcast(I32),
+                w1_scales[:, 4 * q : 4 * q + 4, :].rearrange("a r c -> r a c").bitcast(I32),
+            )
+        gain_c = load_column(gain, "gain_c")
+        mean_c = load_column(mean, "mean_c")
+        idx3 = load_list(offs3, "idx3")
 
-        v_w = [gather(tab_w[0][:].bitcast(U32), idx, U32, "v_w0")]
-        v_s = ring.tile([P, S], U8, name="v_s", tag="wide", align_bytes=64)
-        nc.vector.tensor_copy(v_s[:], tab_s[:].indirect(idx[:]))
-        nc.scalar.dma_start(v_s_hi[0 : P - 4, :].bitcast(I32), v_s[4:P, :].bitcast(I32))
-        w1_w = tile([P, PASSES, 2 * H], U8, "w1_w")
-        nc.vector.tensor_copy(
-            w1_w[:].bitcast(U16).rearrange("p a (t m) -> p a t m", t=PACK),
-            w1_raw[:].bitcast(U16).rearrange("p a (m t) -> p a t m", t=PACK),
-        )
-        w1_s = tile([P, PASSES, H], U8, "w1_s")
-        nc.vector.tensor_copy(
-            w1_s[:].rearrange("p a (t m) -> p a t m", t=PACK),
-            w1_s_raw[:].rearrange("p (a m t) -> p a t m", a=PASSES, t=PACK),
-        )
-        v_w.append(gather(tab_w[1][:].bitcast(U32), idx, U32, "v_w1"))
+        v2_w = [gather(tab2_w[0][:].bitcast(U32), idx2, U32, "v2_w0")]
+        v2_w.append(gather(tab2_w[1][:].bitcast(U32), idx2, U32, "v2_w1"))
         v2_s = gather(tab2_s[:], idx2, U8, "v2_s")
-        v2_w = [gather(tab2_w[a][:].bitcast(U32), idx2, U32, "v2_w%d" % a) for a in range(PASSES)]
-        pages = [tile([P, T2], F32, "page%d" % t) for t in range(PACK)]
-        neg_mean = tile([P, PACK], F32, "neg_mean")
-        nc.scalar.activation(neg_mean[:], mean_c[:], ACT.Copy, scale=-1.0)
+        weave2_tags = ["tab2_s", "w3_raw", "w2_g0", "w2_g1"]
+        weave2 = [load_weave(wg2, 0, "weave2_0", weave2_tags[0])]
+        v_w = [gather(tab_w[0][:].bitcast(U32), idx, U32, "v_w0")]
 
-        def product(tag, bufs, cols, lhs_codes, lhs_scales, rhs_codes, rhs_scales):
-            acc = psum.tile([P, BANK], F32, name=tag, bufs=bufs)
-            for a in range(PASSES):
-                nc.tensor.matmul_mx(
-                    out=acc[:], lhsT=lhs_codes[a], lhsT_scale=lhs_scales[a],
-                    rhs=rhs_codes[a][:, cols].bitcast(FP8X4), rhs_scale=rhs_scales[a][:, cols],
-                    start=(a == 0), stop=(a == PASSES - 1),
-                )
-            return acc
-
-        halves = [slice(j0, j0 + BANK) for j0 in range(0, S, BANK)]
-        planes2 = [v2_s[4 * a : P, :] for a in range(PASSES)]
-
-        def pair_tiles(name):
-            pairs = [ring.tile([P, 2, S], F32, name=name, tag="wide", align_bytes=64) for u in range(PACK // 2)]
-            return [pairs[t // 2][:, t % 2, :] for t in range(PACK)]
-
-        def signed_square(t):
-            ch = slice(P * t, P * (t + 1))
-            codes = [w1_w[:, a, 2 * P * t : 2 * P * (t + 1)].bitcast(FP4X4) for a in range(PASSES)]
-            scales = [w1_s[:, a, ch] for a in range(PASSES)]
-            h = ring.tile([P, S], F32, name="h", bufs=3)
-            for cols in halves:
-                acc = product("acc", 6, cols, codes, scales, v_w, [v_s[:], v_s_hi[:]])
-                nc.scalar.activation(mag[t][:, cols], acc[:], ACT.Abs)
-                nc.vector.scalar_tensor_tensor(h[:, cols], acc[:], gain_c[:, t : t + 1], mag[t][:, cols], ALU.mult, ALU.mult)
-            return h
-
-        def tanh_gate(t):
-            ch = slice(P * t, P * (t + 1))
-            for cols in halves:
-                acc = product("acc_b", 2, cols, [w2_w[a][:, ch].bitcast(FP8X4) for a in range(PASSES)],
-                              [w2_s[a][:, ch] for a in range(PASSES)], v2_w, planes2)
-                nc.scalar.activation(gate[t][:, cols], acc[:], ACT.Tanh)
-
-        def gated_product(t):
-            ch = slice(P * t, P * (t + 1))
-            h = ring.tile([P, S], F32, name="h", bufs=3)
-            for cols in halves:
-                acc = product("acc", 6, cols, [w3_w[:, a, ch].bitcast(FP8X4) for a in range(PASSES)],
-                              [w3_s[4 * a : P, ch] for a in range(PASSES)], v2_w, planes2)
-                nc.vector.tensor_tensor(h[:, cols], acc[:], gate[t][:, cols], ALU.mult)
-            return h
-
-        def scatter(t, lst, h, weave):
-            nc.vector.tensor_tensor(pages[t][:].indirect(lst[:]), h[:], weave[t][:], ALU.mult)
-
-        chunks = [slice(m0, m0 + BANK) for m0 in range(0, T2, BANK)]
-        z = [tile([P, BANK, PACK], BF16, "z%d" % c) for c in range(len(chunks))]
-
-        def centre_on_scalar(t, c):
-            width = 2 if t == PACK - 2 else 1
-            nc.scalar.activation(
-                z[c][:, :, t : t + width], pages[t][:, chunks[c]].unsqueeze(2).to_broadcast([P, BANK, width]),
-                ACT.Identity, bias=neg_mean[:, t : t + 1],
+        w2_g = []
+        for a in range(PASSES):
+            w2_g.append(tile([P, H * PACK], BF16, "w2_g%d" % a))
+            nc.scalar.copy(
+                w2_g[a][:].rearrange("p (t m j) -> p m t j", t=PACK, j=PACK),
+                w2_raw[a][:].rearrange("p j (m t) -> p m t j", t=PACK),
             )
 
-        mag = pair_tiles("mag")
-        gate = pair_tiles("gate")
-        h1 = [signed_square(0), signed_square(1)]
-        scatter(0, idx3, h1[0], weave1)
+        halves = [slice(j0, j0 + BANK) for j0 in range(0, S, BANK)]
+        gates = [tile([P, 2, S], F32, "gate%d" % u, tag="tab2_w%d" % u) for u in range(PACK // 2)]
+
+        def pass_on_v2(acc, a, codes, scales, cols):
+            nc.tensor.matmul_mx(
+                out=acc[:], lhsT=codes.bitcast(FP8X4), lhsT_scale=scales,
+                rhs=v2_w[a][:, cols].bitcast(FP8X4), rhs_scale=v2_s[4 * a : P, cols],
+                start=(a == 0), stop=(a == PASSES - 1),
+            )
+
+        def pass_b(acc, a, t, cols):
+            ch = slice(P * t, P * (t + 1))
+            pass_on_v2(acc, a, w2_q[a][0][:, ch], w2_q[a][1][:, ch], cols)
+            if a == PASSES - 1:
+                nc.scalar.activation(gates[t // 2][:, t % 2, cols], acc[:], ACT.Tanh)
+
+        def bank_b():
+            return psum.tile([P, BANK], F32, name="acc_b", tag="emptied_by_scalar")
+
+        def product_d(t, cols):
+            ch = slice(P * t, P * (t + 1))
+            acc = psum.tile([P, BANK], F32, name="acc_d", bufs=4)
+            for a in range(PASSES):
+                pass_on_v2(acc, a, w3_w[:, a, ch], w3_s[4 * a : P, ch], cols)
+            return acc
+
+        def plane_products(t):
+            banks = []
+            for cols in halves:
+                acc = bank_b()
+                for a in range(PASSES):
+                    pass_b(acc, a, t, cols)
+                banks.append(product_d(t, cols))
+            return banks
+
+        w2_q = [quantise(w2_g[0][:], H, "w2_0")]
+        first_b = [bank_b() for cols in halves]
+        for acc, cols in zip(first_b, halves):
+            pass_b(acc, 0, 0, cols)
+        v_s = gather(tab_s[:], idx, U8, "v_s")
+        nc.gpsimd.dma_start(v_s_hi[0:112, :].bitcast(I32), v_s[4:116, :].bitcast(I32))
+        w1_w = tile([P, PASSES, 2 * H], U8, "w1_w", "tab_s")
+        nc.sync.dma_start(w1_w[:].bitcast(I32), w1_words.rearrange("a p c -> p a c").bitcast(I32))
         w3_w = tile([P, PASSES, H], I32, "w3_w")
         nc.vector.tensor_copy(
             w3_w[:].rearrange("p a (t c i) -> p a c t i", t=PACK, i=4),
@@ -198,72 +187,123 @@ def tile_list_subgrid_closure_weave_kernel(
             w3_s[:].rearrange("p (t m) -> p t m", t=PACK),
             w3_s_raw[:].rearrange("p (m t) -> p t m", t=PACK),
         )
+        w2_q.append(quantise(w2_g[1][:], H, "w2_1"))
+        banks = [[]]
+        for acc, cols in zip(first_b, halves):
+            banks[0].append(product_d(0, cols))
+            pass_b(acc, 1, 0, cols)
+        v_w.append(gather(tab_w[1][:].bitcast(U32), idx, U32, "v_w1"))
 
-        w2_w, w2_s = [], []
-        for a in range(PASSES):
-            grouped = tile([P, H * PACK], BF16, "w2_g%d" % a)
-            nc.scalar.copy(
-                grouped[:].rearrange("p (t m j) -> p m t j", t=PACK, j=PACK),
-                w2_raw[a][:].rearrange("p j (m t) -> p m t j", t=PACK),
-            )
-            w2_w.append(tile([P, H], U32, "w2_w%d" % a))
-            w2_s.append(tile([P, H], U8, "w2_s%d" % a))
-            nc.vector.quantize_mx(out=w2_w[a][:].bitcast(FP8X4), scales=w2_s[a][:], in_=grouped[:])
+        weave2.extend(load_weave(wg2, t, "weave2_%d" % t, weave2_tags[t]) for t in range(1, PACK))
+        pages = [tile([P, T2], F32, "page%d" % t) for t in range(PACK)]
 
-        h1.append(signed_square(2))
-        scatter(1, idx3, h1[1], weave1)
-        h1.append(signed_square(3))
+        def gated(t, banks):
+            h = held.tile([P, S], F32, name="h2", bufs=3)
+            for cols, acc in zip(halves, banks):
+                nc.vector.tensor_tensor(h[:, cols], acc[:], gates[t // 2][:, t % 2, cols], ALU.mult)
+            return h
+
+        def scatter(t, lst, h, weave):
+            nc.vector.tensor_tensor(pages[t][:].indirect(lst[:]), h[:], weave[t][:], ALU.mult)
+
+        v_planes = [v_s, v_s_hi]
+        term_tags = ["tab_w0", "w2_raw0", "w2_raw1", "tab_w1"]
+        terms = [tile([P, 2, 2, H], F32, "terms%d" % u, tag=term_tags[u]) for u in range(len(term_tags))]
+        h1 = [tile([P, S], F32, "h1_%d" % t) for t in range(PACK)]
+
+        def square_and_relu(u):
+            for e in range(2):
+                cells = slice(P * (2 * u + e), P * (2 * u + e + 1))
+                acc = psum.tile([P, BANK], F32, name="acc_a")
+                product(acc, [v_w[a][:, cells].bitcast(FP8X4) for a in range(PASSES)],
+                        [v_planes[a][:, cells] for a in range(PASSES)],
+                        [w1_w[:, a, :].bitcast(FP4X4) for a in range(PASSES)],
+                        [w1_s[:, H * a : H * (a + 1)] for a in range(PASSES)])
+                by_plane = acc[:].rearrange("p (m t) -> p t m", t=PACK)
+                for k, func, scale in ((0, ACT.Square, 1.0), (1, ACT.Relu, -1.0)):
+                    nc.scalar.activation(terms[u][:, k, e, :].rearrange("p (t m) -> p t m", t=PACK), by_plane, func, scale=scale)
+
+        def square_negative_part(u):
+            nc.scalar.activation(terms[u][:, 1], terms[u][:, 1], ACT.Square)
+
+        def scale_negative_part(u):
+            nc.scalar.activation(terms[u][:, 1], terms[u][:, 1], ACT.Copy, scale=-2.0)
+
+        def turn(t, half):
+            acc = psum.tile([P, BANK], F32, name="acc_x", tag="emptied_by_scalar")
+            for i in range(BANK // P):
+                u, e = divmod(half * (BANK // P) + i, 2)
+                for k in range(2):
+                    nc.tensor.matmul(acc[:, P * i : P * (i + 1)], lhsT=terms[u][:, k, e, P * t : P * (t + 1)], rhs=ident[:],
+                                     is_transpose=True, start=(k == 0), stop=(k == 1))
+            nc.scalar.activation(h1[t][:, halves[half]], acc[:], ACT.Copy, scale=gain_c[:, t : t + 1])
+
+        h2 = [gated(0, banks[0])]
+        banks.append(plane_products(1))
+        scatter(0, idx4, h2[0], weave2)
+        h2.append(gated(1, banks[1]))
+        for t in range(1, PACK):
+            if t + 1 < PACK:
+                banks.append(plane_products(t + 1))
+                h2.append(gated(t + 1, banks[t + 1]))
+            scatter(t, idx4, h2[t], weave2)
+
+        weave1_tags = ["v2_w0", "v2_w1", "w3_w", "w2_0_w"]
+        weave1 = [load_weave(wg1, t, "weave1_%d" % t, weave1_tags[t]) for t in range(PACK)]
+        w4_raw = load_rows(w4, N, "w4_raw", "w2_1_w")
+        for u in range(len(terms)):
+            square_and_relu(u)
+            if u > 0:
+                scale_negative_part(u - 1)
+            square_negative_part(u)
+            if u == 2:
+                for t in range(PACK):
+                    turn(t, 0)
+        neg_mean = tile([P, PACK], F32, "neg_mean")
+        nc.scalar.activation(neg_mean[:], mean_c[:], ACT.Copy, scale=-1.0)
+        scale_negative_part(len(terms) - 1)
         for t in range(PACK):
-            tanh_gate(t)
-        scatter(2, idx3, h1[2], weave1)
-        h2 = [gated_product(0)]
-        scatter(3, idx3, h1[3], weave1)
+            turn(t, 1)
+
         w4_g = tile([P, N * PACK], BF16, "w4_g")
         nc.scalar.copy(
             w4_g[:].rearrange("p (c i j) -> p c j i", i=4, j=PACK),
             w4_raw[:].rearrange("p j (c i) -> p c j i", i=4),
         )
-        w4_w = tile([P, N], U32, "w4_w")
-        w4_s = tile([P, N], U8, "w4_s")
-        nc.vector.quantize_mx(out=w4_w[:].bitcast(FP8X4), scales=w4_s[:], in_=w4_g[:])
+
+        chunks = [slice(m0, m0 + BANK) for m0 in range(0, T2, BANK)]
+        z = [tile([P, BANK, PACK], BF16, "z%d" % c) for c in range(len(chunks))]
+        last = PACK - 1
+
+        def centre_on_scalar(t, c):
+            width = 2 if t == last - 1 else 1
+            nc.scalar.activation(
+                z[c][:, :, t : t + width], pages[t][:, chunks[c]].unsqueeze(2).to_broadcast([P, BANK, width]),
+                ACT.Identity, bias=neg_mean[:, t : t + 1],
+            )
+
+        def centre_on_vector(t, c):
+            nc.vector.tensor_scalar(z[c][:, :, t], pages[t][:, chunks[c]], mean_c[:, t : t + 1], None, ALU.subtract)
 
         for t in range(PACK):
-            if t + 1 < PACK:
-                h2.append(gated_product(t + 1))
-            scatter(t, idx4, h2[t], weave2)
-        for t in range(PACK - 1):
+            scatter(t, idx3, h1[t], weave1)
+            if t == 1:
+                w4_w, w4_s = quantise(w4_g[:], N, "w4")
+        for t in range(last):
             for c in range(len(chunks)):
                 centre_on_scalar(t, c)
+        for c in range(len(chunks)):
+            (centre_on_vector if c < 2 else centre_on_scalar)(last, c)
 
-        last = PACK - 1
-        centre_on_scalar(last, 2)
-        centre_on_scalar(last, 3)
-
-        def centre_last(c):
-            nc.vector.tensor_scalar(z[c][:, :, last], pages[last][:, chunks[c]], mean_c[:, last : last + 1], None, ALU.subtract)
-
-        def quantise(c):
-            z_w = tile([P, BANK], U32, "z_w%d" % c)
-            z_s = tile([P, BANK], U8, "z_s%d" % c)
-            nc.vector.quantize_mx(out=z_w[:].bitcast(FP8X4), scales=z_s[:], in_=z[c][:].rearrange("p m t -> p (m t)"))
-            return z_w, z_s
-
-        def finish(c, z_w, z_s):
-            for n0 in range(0, N, P):
-                acc = psum.tile([P, BANK], F32, name="acc", bufs=6)
-                nc.tensor.matmul_mx(
-                    out=acc[:], lhsT=w4_w[:, n0 : n0 + P].bitcast(FP8X4), lhsT_scale=w4_s[:, n0 : n0 + P],
-                    rhs=z_w[:].bitcast(FP8X4), rhs_scale=z_s[:], start=True, stop=True,
-                )
-                res = ring.tile([P, BANK], F32, name="res", bufs=8)
-                if c > 0 and n0:
-                    nc.vector.tensor_copy(res[:], acc[:])
+        z_q = [quantise(z[c][:].rearrange("p m t -> p (m t)"), BANK, "z%d" % c) for c in range(len(chunks))]
+        for c, (z_w, z_s) in enumerate(z_q):
+            res = tile([P, N // P, BANK], F32, "res%d" % c, tag=weave2_tags[c])
+            for h in range(N // P):
+                rows = slice(P * h, P * (h + 1))
+                acc = psum.tile([P, BANK], F32, name="acc_d", bufs=4)
+                product(acc, [w4_w[:, rows].bitcast(FP8X4)], [w4_s[:, rows]], [z_w[:].bitcast(FP8X4)], [z_s[:]])
+                if c > 0 and h:
+                    nc.vector.tensor_copy(res[:, h, :], acc[:])
                 else:
-                    nc.scalar.copy(res[:], acc[:])
-                nc.sync.dma_start(out[n0 : n0 + P, chunks[c]], res[:])
-
-        centre_last(0)
-        centre_last(1)
-        quantised = [quantise(c) for c in range(len(chunks))]
-        for c, (z_w, z_s) in enumerate(quantised):
-            finish(c, z_w, z_s)
+                    nc.scalar.copy(res[:, h, :], acc[:])
+                nc.sync.dma_start(out[rows, chunks[c]], res[:, h, :])

@@ -68,7 +68,8 @@ def tile_list_subgrid_closure_weave_kernel(
         def load_weave(src, t, name, tag):
             dst = tile([P, S], F32, name, tag)
             rows = src.rearrange("(q t) j -> t q j", t=PACK)[t]
-            nc.sync.dma_start(dst[:], rows.unsqueeze(0).to_broadcast([QUADS, 32, S]))
+            for q in range(QUADS):
+                nc.sync.dma_start(dst[32 * q : 32 * (q + 1), :], rows)
             return dst
 
         def gather(window, lst, dtype, name):
@@ -130,8 +131,8 @@ def tile_list_subgrid_closure_weave_kernel(
         for a in range(PASSES):
             w2_g.append(tile([P, H * PACK], BF16, "w2_g%d" % a))
             nc.scalar.copy(
-                w2_g[a][:].rearrange("p (t m j) -> p m t j", t=PACK, j=PACK),
-                w2_raw[a][:].rearrange("p j (m t) -> p m t j", t=PACK),
+                w2_g[a][:].rearrange("p (t m j) -> p t m j", t=PACK, j=PACK),
+                w2_raw[a][:].rearrange("p j (m t) -> p t m j", t=PACK),
             )
 
         halves = [slice(j0, j0 + BANK) for j0 in range(0, S, BANK)]
@@ -219,9 +220,9 @@ def tile_list_subgrid_closure_weave_kernel(
                         [v_planes[a][:, cells] for a in range(PASSES)],
                         [w1_w[:, a, :].bitcast(FP4X4) for a in range(PASSES)],
                         [w1_s[:, H * a : H * (a + 1)] for a in range(PASSES)])
-                by_plane = acc[:].rearrange("p (m t) -> p t m", t=PACK)
+                by_plane = acc[:].rearrange("p (c i t) -> p c t i", i=4, t=PACK)
                 for k, func, scale in ((0, ACT.Square, 1.0), (1, ACT.Relu, -1.0)):
-                    nc.scalar.activation(terms[u][:, k, e, :].rearrange("p (t m) -> p t m", t=PACK), by_plane, func, scale=scale)
+                    nc.scalar.activation(terms[u][:, k, e, :].rearrange("p (t c i) -> p c t i", t=PACK, i=4), by_plane, func, scale=scale)
 
         def square_negative_part(u):
             nc.scalar.activation(terms[u][:, 1], terms[u][:, 1], ACT.Square)
@@ -275,25 +276,31 @@ def tile_list_subgrid_closure_weave_kernel(
         z = [tile([P, BANK, PACK], BF16, "z%d" % c) for c in range(len(chunks))]
         last = PACK - 1
 
-        def centre_on_scalar(t, c):
-            width = 2 if t == last - 1 else 1
-            nc.scalar.activation(
-                z[c][:, :, t : t + width], pages[t][:, chunks[c]].unsqueeze(2).to_broadcast([P, BANK, width]),
-                ACT.Identity, bias=neg_mean[:, t : t + 1],
-            )
+        def centre_on_scalar(t, c, bias):
+            nc.scalar.activation(z[c][:, :, t], pages[t][:, chunks[c]], ACT.Identity, bias=bias)
 
-        def centre_on_vector(t, c):
-            nc.vector.tensor_scalar(z[c][:, :, t], pages[t][:, chunks[c]], mean_c[:, t : t + 1], None, ALU.subtract)
+        def negate_mean(dst, t0, t1):
+            nc.scalar.activation(dst, mean_c[:, t0:t1], ACT.Copy, scale=-1.0)
+
+        handed = tile([P, 1], F32, "handed")
+        negate_mean(handed[:], last - 1, last)
 
         for t in range(PACK):
             scatter(t, idx3, h1[t], weave1)
             if t == 1:
                 w4_w, w4_s = quantise(w4_g[:], N, "w4")
+        on_vector = 2
         for t in range(last):
             for c in range(len(chunks)):
-                centre_on_scalar(t, c)
+                shared = t == last - 1 and c < on_vector
+                centre_on_scalar(t, c, handed[:] if shared else neg_mean[:, t : t + 1])
+                if shared and c == on_vector - 1:
+                    negate_mean(handed[:], last, PACK)
         for c in range(len(chunks)):
-            (centre_on_vector if c < 2 else centre_on_scalar)(last, c)
+            if c < on_vector:
+                nc.vector.tensor_scalar(z[c][:, :, last], pages[last][:, chunks[c]], handed[:], None, ALU.add)
+            else:
+                centre_on_scalar(last, c, neg_mean[:, last:PACK])
 
         z_q = [quantise(z[c][:].rearrange("p m t -> p (m t)"), BANK, "z%d" % c) for c in range(len(chunks))]
         for c, (z_w, z_s) in enumerate(z_q):

@@ -156,7 +156,7 @@ def tile_list_subgrid_closure_weave_kernel(
 
         def product_d(t, cols):
             ch = slice(P * t, P * (t + 1))
-            acc = psum.tile([P, BANK], F32, name="acc_d", bufs=4)
+            acc = psum.tile([P, BANK], F32, name="acc_d", bufs=6)
             for a in range(PASSES):
                 pass_on_v2(acc, a, w3_w[:, a, ch], w3_s[4 * a : P, ch], cols)
             return acc
@@ -215,7 +215,7 @@ def tile_list_subgrid_closure_weave_kernel(
         def square_and_relu(u):
             for e in range(2):
                 cells = slice(P * (2 * u + e), P * (2 * u + e + 1))
-                acc = psum.tile([P, BANK], F32, name="acc_a")
+                acc = psum.tile([P, BANK], F32, name="acc_a", tag="emptied_by_scalar")
                 product(acc, [v_w[a][:, cells].bitcast(FP8X4) for a in range(PASSES)],
                         [v_planes[a][:, cells] for a in range(PASSES)],
                         [w1_w[:, a, :].bitcast(FP4X4) for a in range(PASSES)],
@@ -258,22 +258,24 @@ def tile_list_subgrid_closure_weave_kernel(
                 scale_negative_part(u - 1)
             square_negative_part(u)
             if u == 2:
-                for t in range(PACK):
-                    turn(t, 0)
-        neg_mean = tile([P, PACK], F32, "neg_mean")
-        nc.scalar.activation(neg_mean[:], mean_c[:], ACT.Copy, scale=-1.0)
+                turn(0, 0)
         scale_negative_part(len(terms) - 1)
-        for t in range(PACK):
-            turn(t, 1)
+        turn(0, 1)
+        for t in range(1, PACK):
+            for half in range(len(halves)):
+                turn(t, half)
 
+        neg_mean = gain_c
+        nc.scalar.activation(neg_mean[:], mean_c[:], ACT.Copy, scale=-1.0)
         w4_g = tile([P, N * PACK], BF16, "w4_g")
         nc.scalar.copy(
             w4_g[:].rearrange("p (c i j) -> p c j i", i=4, j=PACK),
             w4_raw[:].rearrange("p j (c i) -> p c j i", i=4),
         )
 
-        chunks = [slice(m0, m0 + BANK) for m0 in range(0, T2, BANK)]
-        z = [tile([P, BANK, PACK], BF16, "z%d" % c) for c in range(len(chunks))]
+        widths = [BANK] * 4
+        chunks = [slice(sum(widths[:c]), sum(widths[: c + 1])) for c in range(len(widths))]
+        z = [tile([P, widths[c], PACK], BF16, "z%d" % c) for c in range(len(chunks))]
         last = PACK - 1
 
         def centre_on_scalar(t, c, bias):
@@ -282,34 +284,42 @@ def tile_list_subgrid_closure_weave_kernel(
         def negate_mean(dst, t0, t1):
             nc.scalar.activation(dst, mean_c[:, t0:t1], ACT.Copy, scale=-1.0)
 
-        handed = tile([P, 1], F32, "handed")
-        negate_mean(handed[:], last - 1, last)
+        on_vector = 2
+        handed = [tile([P, 1], F32, "handed%d" % c) for c in range(on_vector)]
+        for c in range(on_vector):
+            negate_mean(handed[c][:], last - 1, last)
 
         for t in range(PACK):
             scatter(t, idx3, h1[t], weave1)
             if t == 1:
                 w4_w, w4_s = quantise(w4_g[:], N, "w4")
-        on_vector = 2
         for t in range(last):
             for c in range(len(chunks)):
-                shared = t == last - 1 and c < on_vector
-                centre_on_scalar(t, c, handed[:] if shared else neg_mean[:, t : t + 1])
-                if shared and c == on_vector - 1:
-                    negate_mean(handed[:], last, PACK)
-        for c in range(len(chunks)):
-            if c < on_vector:
-                nc.vector.tensor_scalar(z[c][:, :, last], pages[last][:, chunks[c]], handed[:], None, ALU.add)
-            else:
-                centre_on_scalar(last, c, neg_mean[:, last:PACK])
+                if t == last - 1 and c < on_vector:
+                    centre_on_scalar(t, c, handed[c][:])
+                    negate_mean(handed[c][:], last, PACK)
+                else:
+                    centre_on_scalar(t, c, neg_mean[:, t : t + 1])
+        for c in range(on_vector, len(chunks)):
+            centre_on_scalar(last, c, neg_mean[:, last:PACK])
 
-        z_q = [quantise(z[c][:].rearrange("p m t -> p (m t)"), BANK, "z%d" % c) for c in range(len(chunks))]
+        def centre_on_vector(c):
+            nc.vector.tensor_scalar(z[c][:, :, last], pages[last][:, chunks[c]], handed[c][:], None, ALU.add)
+
+        z_q = []
+        centre_on_vector(0)
+        for c in range(len(chunks)):
+            if c + 1 < on_vector:
+                centre_on_vector(c + 1)
+            z_q.append(quantise(z[c][:].rearrange("p m t -> p (m t)"), widths[c], "z%d" % c))
+        res_tags = weave2_tags + ["h1_0"]
         for c, (z_w, z_s) in enumerate(z_q):
-            res = tile([P, N // P, BANK], F32, "res%d" % c, tag=weave2_tags[c])
+            res = tile([P, N // P, widths[c]], F32, "res%d" % c, tag=res_tags[c])
             for h in range(N // P):
                 rows = slice(P * h, P * (h + 1))
-                acc = psum.tile([P, BANK], F32, name="acc_d", bufs=4)
+                acc = psum.tile([P, widths[c]], F32, name="acc_d", bufs=6)
                 product(acc, [w4_w[:, rows].bitcast(FP8X4)], [w4_s[:, rows]], [z_w[:].bitcast(FP8X4)], [z_s[:]])
-                if c > 0 and h:
+                if h:
                     nc.vector.tensor_copy(res[:, h, :], acc[:])
                 else:
                     nc.scalar.copy(res[:, h, :], acc[:])

from contextlib import ExitStack

import concourse.mybir as mybir
from concourse.masks import make_identity

K, H, N, T, S, T2 = 1024, 512, 256, 2048, 1024, 2048
FLOPS = 2 * (3 * K * H * S + H * N * T2)

F32 = mybir.dt.float32
BF16 = mybir.dt.bfloat16
I32 = mybir.dt.int32
U32 = mybir.dt.uint32
U16 = mybir.dt.uint16
U8 = mybir.dt.uint8
FP8X4 = mybir.dt.float8_e4m3fn_x4
FP4X4 = mybir.dt.float4_e2m1fn_x4
ACT = mybir.ActivationFunctionType
ALU = mybir.AluOpType

P = 128
PACK = 4
PASSES = K // (P * PACK)
BANK = 512
QUADS = 4


def tile_list_subgrid_closure_weave_kernel(
    tc, tab_words, tab_scales, tab2_words, tab2_scales, w1_words, w1_scales, w2, w3_words, w3_scales,
    w4, gain, mean, wg1, wg2, offs, offs2, offs3, offs4, out,
):
    nc = tc.nc
    with ExitStack() as ctx:
        held = ctx.enter_context(tc.tile_pool(name="held", bufs=1))
        psum = ctx.enter_context(tc.psum_pool(name="psum", bufs=2))

        def tile(shape, dtype, name, tag=None):
            return held.tile(shape, dtype, name=name, tag=tag or name, align_bytes=64)

        def load_list(src, name):
            dst = held.tile([P, S // 16], U16, name=name)
            nc.sync.dma_start(dst[:], src)
            return dst

        def zeroed(shape, name, engine):
            dst = tile(shape, U8, name)
            engine.memset(dst[:].bitcast(I32), 0)
            return dst

        def load_words(src, a, name):
            dst = tile([P, T], I32, name)
            nc.sync.dma_start(dst[:], src[a].rearrange("p n i -> p (n i)").bitcast(I32))
            return dst

        def load_packed_scales(dst, src, queue):
            for q in range(QUADS):
                queue.dma_start(dst[32 * q : 32 * q + 4 * PASSES, :].bitcast(I32), src[:, 4 * q : 4 * q + 4, :].bitcast(I32))

        def load_rows(src, width, name, tag=None):
            dst = tile([P, PACK, width], F32, name, tag)
            nc.sync.dma_start(dst[:], src.rearrange("(p j) c -> p j c", j=PACK))
            return dst

        def load_column(src, name):
            dst = tile([P, PACK], F32, name)
            nc.sync.dma_start(dst[:], src.rearrange("(p t) -> p t", t=PACK))
            return dst

        def load_weave(src, t, name, tag):
            dst = tile([P, S], F32, name, tag)
            rows = src.rearrange("(q t) j -> t q j", t=PACK)[t]
            for q in range(QUADS):
                nc.sync.dma_start(dst[32 * q : 32 * (q + 1), :], rows)
            return dst

        def gather(window, lst, dtype, name):
            dst = tile([P, S], dtype, name)
            nc.vector.tensor_copy(dst[:], window.indirect(lst[:]))
            return dst

        def quantise(grouped, width, name):
            codes = tile([P, width], U32, name + "_w")
            scales = tile([P, width], U8, name + "_s")
            nc.vector.quantize_mx(out=codes[:].bitcast(FP8X4), scales=scales[:], in_=grouped)
            return codes, scales

        def product(acc, lhs_codes, lhs_scales, rhs_codes, rhs_scales):
            for a in range(len(lhs_codes)):
                nc.tensor.matmul_mx(
                    out=acc[:], lhsT=lhs_codes[a], lhsT_scale=lhs_scales[a], rhs=rhs_codes[a], rhs_scale=rhs_scales[a],
                    start=(a == 0), stop=(a == len(lhs_codes) - 1),
                )

        ident = tile([P, P], F32, "ident")
        make_identity(nc, ident[:])
        tab2_s = zeroed([P, T], "tab2_s", nc.vector)
        load_packed_scales(tab2_s, tab2_scales, nc.gpsimd)
        tab_s = zeroed([P, T], "tab_s", nc.vector)
        load_packed_scales(tab_s, tab_scales, nc.gpsimd)
        w3_s_raw = zeroed([P, H], "w3_s_raw", nc.vector)
        w1_s = zeroed([P, PASSES * H], "w1_s", nc.vector)
        v_s_hi = zeroed([P, S], "v_s_hi", nc.vector)

        idx2 = load_list(offs2, "idx2")
        tab2_w = [load_words(tab2_words, a, "tab2_w%d" % a) for a in range(PASSES)]
        idx = load_list(offs, "idx")
        w2_raw = [load_rows(w2[0:512, :], H, "w2_raw0")]
        tab_w = [load_words(tab_words, 0, "tab_w0")]
        w2_raw.append(load_rows(w2[512:1024, :], H, "w2_raw1"))
        w3_raw = tile([P, PASSES, H], I32, "w3_raw")
        nc.sync.dma_start(w3_raw[:], w3_words.rearrange("a p c i -> p a (c i)").bitcast(I32))
        load_packed_scales(w3_s_raw, w3_scales, nc.sync)
        tab_w.append(load_words(tab_words, 1, "tab_w1"))
        idx4 = load_list(offs4, "idx4")
        for q in range(QUADS):
            nc.sync.dma_start(
                w1_s[32 * q : 32 * q + 4, :].rearrange("r (a c) -> r a c", a=PASSES).bitcast(I32),
                w1_scales[:, 4 * q : 4 * q + 4, :].rearrange("a r c -> r a c").bitcast(I32),
            )
        gain_c = load_column(gain, "gain_c")
        mean_c = load_column(mean, "mean_c")
        idx3 = load_list(offs3, "idx3")

        v2_w = [gather(tab2_w[0][:].bitcast(U32), idx2, U32, "v2_w0")]
        v2_w.append(gather(tab2_w[1][:].bitcast(U32), idx2, U32, "v2_w1"))
        v2_s = gather(tab2_s[:], idx2, U8, "v2_s")
        weave2_tags = ["tab2_s", "w3_raw", "w2_g0", "w2_g1"]
        weave2 = [load_weave(wg2, 0, "weave2_0", weave2_tags[0])]
        v_w = [gather(tab_w[0][:].bitcast(U32), idx, U32, "v_w0")]

        w2_g = []
        for a in range(PASSES):
            w2_g.append(tile([P, H * PACK], BF16, "w2_g%d" % a))
            nc.scalar.copy(
                w2_g[a][:].rearrange("p (t m j) -> p t m j", t=PACK, j=PACK),
                w2_raw[a][:].rearrange("p j (m t) -> p t m j", t=PACK),
            )

        halves = [slice(j0, j0 + BANK) for j0 in range(0, S, BANK)]
        gates = [tile([P, 2, S], F32, "gate%d" % u, tag="tab2_w%d" % u) for u in range(PACK // 2)]

        def pass_on_v2(acc, a, codes, scales, cols):
            nc.tensor.matmul_mx(
                out=acc[:], lhsT=codes.bitcast(FP8X4), lhsT_scale=scales,
                rhs=v2_w[a][:, cols].bitcast(FP8X4), rhs_scale=v2_s[4 * a : P, cols],
                start=(a == 0), stop=(a == PASSES - 1),
            )

        def pass_b(acc, a, t, cols):
            ch = slice(P * t, P * (t + 1))
            pass_on_v2(acc, a, w2_q[a][0][:, ch], w2_q[a][1][:, ch], cols)
            if a == PASSES - 1:
                nc.scalar.activation(gates[t // 2][:, t % 2, cols], acc[:], ACT.Tanh)

        def bank_b():
            return psum.tile([P, BANK], F32, name="acc_b", tag="emptied_by_scalar")

        def product_d(t, cols):
            ch = slice(P * t, P * (t + 1))
            acc = psum.tile([P, BANK], F32, name="acc_d", bufs=6)
            for a in range(PASSES):
                pass_on_v2(acc, a, w3_w[:, a, ch], w3_s[4 * a : P, ch], cols)
            return acc

        def plane_products(t):
            banks = []
            for cols in halves:
                acc = bank_b()
                for a in range(PASSES):
                    pass_b(acc, a, t, cols)
                banks.append(product_d(t, cols))
            return banks

        w2_q = [quantise(w2_g[0][:], H, "w2_0")]
        first_b = [bank_b() for cols in halves]
        for acc, cols in zip(first_b, halves):
            pass_b(acc, 0, 0, cols)
        v_s = gather(tab_s[:], idx, U8, "v_s")
        nc.gpsimd.dma_start(v_s_hi[0:112, :].bitcast(I32), v_s[4:116, :].bitcast(I32))
        w1_w = tile([P, PASSES, 2 * H], U8, "w1_w", "tab_s")
        nc.sync.dma_start(w1_w[:].bitcast(I32), w1_words.rearrange("a p c -> p a c").bitcast(I32))
        w3_w = tile([P, PASSES, H], I32, "w3_w")
        nc.vector.tensor_copy(
            w3_w[:].rearrange("p a (t c i) -> p a c t i", t=PACK, i=4),
            w3_raw[:].rearrange("p a (c i t) -> p a c t i", t=PACK, i=4),
        )
        w3_s = tile([P, H], U8, "w3_s")
        nc.vector.tensor_copy(
            w3_s[:].rearrange("p (t m) -> p t m", t=PACK),
            w3_s_raw[:].rearrange("p (m t) -> p t m", t=PACK),
        )
        w2_q.append(quantise(w2_g[1][:], H, "w2_1"))
        banks = [[]]
        for acc, cols in zip(first_b, halves):
            banks[0].append(product_d(0, cols))
            pass_b(acc, 1, 0, cols)
        v_w.append(gather(tab_w[1][:].bitcast(U32), idx, U32, "v_w1"))

        weave2.extend(load_weave(wg2, t, "weave2_%d" % t, weave2_tags[t]) for t in range(1, PACK))
        pages = [tile([P, T2], F32, "page%d" % t) for t in range(PACK)]

        def gated(t, banks):
            h = held.tile([P, S], F32, name="h2", bufs=3)
            for cols, acc in zip(halves, banks):
                nc.vector.tensor_tensor(h[:, cols], acc[:], gates[t // 2][:, t % 2, cols], ALU.mult)
            return h

        def scatter(t, lst, h, weave):
            nc.vector.tensor_tensor(pages[t][:].indirect(lst[:]), h[:], weave[t][:], ALU.mult)

        v_planes = [v_s, v_s_hi]
        term_tags = ["tab_w0", "w2_raw0", "w2_raw1", "tab_w1"]
        terms = [tile([P, 2, 2, H], F32, "terms%d" % u, tag=term_tags[u]) for u in range(len(term_tags))]
        h1 = [tile([P, S], F32, "h1_%d" % t) for t in range(PACK)]

        def square_and_relu(u):
            for e in range(2):
                cells = slice(P * (2 * u + e), P * (2 * u + e + 1))
                acc = psum.tile([P, BANK], F32, name="acc_a", tag="emptied_by_scalar")
                product(acc, [v_w[a][:, cells].bitcast(FP8X4) for a in range(PASSES)],
                        [v_planes[a][:, cells] for a in range(PASSES)],
                        [w1_w[:, a, :].bitcast(FP4X4) for a in range(PASSES)],
                        [w1_s[:, H * a : H * (a + 1)] for a in range(PASSES)])
                by_plane = acc[:].rearrange("p (c i t) -> p c t i", i=4, t=PACK)
                for k, func, scale in ((0, ACT.Square, 1.0), (1, ACT.Relu, -1.0)):
                    nc.scalar.activation(terms[u][:, k, e, :].rearrange("p (t c i) -> p c t i", t=PACK, i=4), by_plane, func, scale=scale)

        def square_negative_part(u):
            nc.scalar.activation(terms[u][:, 1], terms[u][:, 1], ACT.Square)

        def scale_negative_part(u):
            nc.scalar.activation(terms[u][:, 1], terms[u][:, 1], ACT.Copy, scale=-2.0)

        def turn(t, half):
            acc = psum.tile([P, BANK], F32, name="acc_x", tag="emptied_by_scalar")
            for i in range(BANK // P):
                u, e = divmod(half * (BANK // P) + i, 2)
                for k in range(2):
                    nc.tensor.matmul(acc[:, P * i : P * (i + 1)], lhsT=terms[u][:, k, e, P * t : P * (t + 1)], rhs=ident[:],
                                     is_transpose=True, start=(k == 0), stop=(k == 1))
            nc.scalar.activation(h1[t][:, halves[half]], acc[:], ACT.Copy, scale=gain_c[:, t : t + 1])

        h2 = [gated(0, banks[0])]
        banks.append(plane_products(1))
        scatter(0, idx4, h2[0], weave2)
        h2.append(gated(1, banks[1]))
        for t in range(1, PACK):
            if t + 1 < PACK:
                banks.append(plane_products(t + 1))
                h2.append(gated(t + 1, banks[t + 1]))
            scatter(t, idx4, h2[t], weave2)

        weave1_tags = ["v2_w0", "v2_w1", "w3_w", "w2_0_w"]
        weave1 = [load_weave(wg1, t, "weave1_%d" % t, weave1_tags[t]) for t in range(PACK)]
        w4_raw = load_rows(w4, N, "w4_raw", "w2_1_w")
        for u in range(len(terms)):
            square_and_relu(u)
            if u > 0:
                scale_negative_part(u - 1)
            square_negative_part(u)
            if u == 2:
                turn(0, 0)
        scale_negative_part(len(terms) - 1)
        turn(0, 1)
        for t in range(1, PACK):
            for half in range(len(halves)):
                turn(t, half)

        neg_mean = gain_c
        nc.scalar.activation(neg_mean[:], mean_c[:], ACT.Copy, scale=-1.0)
        w4_g = tile([P, N * PACK], BF16, "w4_g")
        nc.scalar.copy(
            w4_g[:].rearrange("p (c i j) -> p c j i", i=4, j=PACK),
            w4_raw[:].rearrange("p j (c i) -> p c j i", i=4),
        )

        widths = [BANK] * 4
        chunks = [slice(sum(widths[:c]), sum(widths[: c + 1])) for c in range(len(widths))]
        z = [tile([P, widths[c], PACK], BF16, "z%d" % c) for c in range(len(chunks))]
        last = PACK - 1

        def centre_on_scalar(t, c, bias):
            nc.scalar.activation(z[c][:, :, t], pages[t][:, chunks[c]], ACT.Identity, bias=bias)

        def negate_mean(dst, t0, t1):
            nc.scalar.activation(dst, mean_c[:, t0:t1], ACT.Copy, scale=-1.0)

        on_vector = 2
        handed = [tile([P, 1], F32, "handed%d" % c) for c in range(on_vector)]
        for c in range(on_vector):
            negate_mean(handed[c][:], last - 1, last)

        for t in range(PACK):
            scatter(t, idx3, h1[t], weave1)
            if t == 1:
                w4_w, w4_s = quantise(w4_g[:], N, "w4")
        for t in range(last):
            for c in range(len(chunks)):
                if t == last - 1 and c < on_vector:
                    centre_on_scalar(t, c, handed[c][:])
                    negate_mean(handed[c][:], last, PACK)
                else:
                    centre_on_scalar(t, c, neg_mean[:, t : t + 1])
        for c in range(on_vector, len(chunks)):
            centre_on_scalar(last, c, neg_mean[:, last:PACK])

        def centre_on_vector(c):
            nc.vector.tensor_scalar(z[c][:, :, last], pages[last][:, chunks[c]], handed[c][:], None, ALU.add)

        z_q = []
        centre_on_vector(0)
        for c in range(len(chunks)):
            if c + 1 < on_vector:
                centre_on_vector(c + 1)
            z_q.append(quantise(z[c][:].rearrange("p m t -> p (m t)"), widths[c], "z%d" % c))
        res_tags = weave2_tags + ["h1_0"]
        for c, (z_w, z_s) in enumerate(z_q):
            res = tile([P, N // P, widths[c]], F32, "res%d" % c, tag=res_tags[c])
            for h in range(N // P):
                rows = slice(P * h, P * (h + 1))
                acc = psum.tile([P, widths[c]], F32, name="acc_d", bufs=6)
                product(acc, [w4_w[:, rows].bitcast(FP8X4)], [w4_s[:, rows]], [z_w[:].bitcast(FP8X4)], [z_s[:]])
                if h:
                    nc.vector.tensor_copy(res[:, h, :], acc[:])
                else:
                    nc.scalar.copy(res[:, h, :], acc[:])
                nc.sync.dma_start(out[rows, chunks[c]], res[:, h, :])
